import numpy as np
import ml_dtypes


def mxq(x, axis, fmt="e4m3"):
    dtype, down = {"e4m3": (ml_dtypes.float8_e4m3fn, 7), "e5m2": (ml_dtypes.float8_e5m2, 14)}[fmt]
    v = np.moveaxis(np.asarray(x, np.float32).astype(ml_dtypes.bfloat16).astype(np.float64), axis, -1)
    blocks = v.reshape(v.shape[:-1] + (-1, 32))
    amax = np.abs(blocks).max(-1, keepdims=True)
    byte = np.maximum(np.where(amax > 0, np.frexp(amax)[1] - 1 + 127, 0) - down, 1)
    scale = np.exp2(byte - 127.0)
    codes = (blocks / scale).astype(np.float32).astype(dtype).astype(np.float64)
    return np.moveaxis((codes * scale).reshape(v.shape), -1, axis)


WIDE = False


def mx_kscale(k):
    if not WIDE:
        return np.ones(k)
    levels = np.array([10, -10, 5, -5, 0])
    if k % 512:
        return np.exp2(np.random.permutation(np.resize(levels, k // 32))).repeat(32)
    a = np.empty((k // 512, 16))
    for p in range(k // 512):
        a[p, :8] = np.random.permutation(np.resize(levels, 8))
        for g in range(8):
            far = levels[np.abs(levels - a[p, g]) >= 10]
            a[p, g + 8] = far[np.random.randint(len(far))]
    return np.exp2(a.ravel()).repeat(32)


def f64(x):
    return np.asarray(x).astype(np.float64)


def striped(idx):
    return np.tile(idx.reshape(-1, 16).T, (8, 1)).astype(np.uint16)


def unstriped(offs):
    return offs[:16].T.reshape(-1).astype(np.int64)


E2M1 = np.array([0.0, 0.5, 1.0, 1.5, 2.0, 3.0, 4.0, 6.0, -0.0, -0.5, -1.0, -1.5, -2.0, -3.0, -4.0, -6.0])


def pack_weight(w, fmt):
    k, n = w.shape
    w = f64(np.asarray(w, np.float32).astype(ml_dtypes.bfloat16)).reshape(k // 32, 32, n)
    amax = np.abs(w).max(1)
    if fmt == "e4m3":
        byte = np.frexp(amax)[1] - 1 + 127 - 7
    else:
        mant, ex = np.frexp(amax / 6.0)
        byte = np.where(mant > 0.5, ex, ex - 1) + 127
    byte = np.clip(np.where(amax > 0, byte, 1), 1, 254)
    scaled = (w * np.exp2(127.0 - byte)[:, None, :]).reshape(k, n).astype(np.float32)
    by_word = np.ascontiguousarray(scaled.reshape(k // 512, 128, 4, n).transpose(0, 1, 3, 2))
    if fmt == "e4m3":
        words = by_word.astype(ml_dtypes.float8_e4m3fn).view(np.uint8)
    else:
        c = by_word.astype(ml_dtypes.float4_e2m1fn).view(np.uint8) & 0xF
        words = (c[..., 0::2] | (c[..., 1::2] << 4)).reshape(k // 512, 128, 2 * n)
    return np.ascontiguousarray(words), np.ascontiguousarray(byte.astype(np.uint8).reshape(k // 512, 16, n))


def unpack_weight(words, scales, fmt):
    g, _, n = scales.shape
    words = np.ascontiguousarray(words).reshape(g, 128, n, -1)
    if fmt == "e4m3":
        vals = words.view(ml_dtypes.float8_e4m3fn).astype(np.float64)
    else:
        nib = np.empty((g, 128, n, 4), np.uint8)
        nib[..., 0::2] = words & 0xF
        nib[..., 1::2] = words >> 4
        vals = E2M1[nib]
    vals = vals * np.repeat(np.exp2(scales.astype(np.float64) - 127.0), 8, axis=1)[..., None]
    return vals.transpose(0, 1, 3, 2).reshape(g * 512, n)


def gelu(v):
    return 0.5 * v * (1.0 + np.tanh(np.sqrt(2.0 / np.pi) * (v + 0.044715 * v**3)))


T, S, P, K, H, N = 2048, 1024, 512, 1024, 1024, 768

def setup_inputs():
    n = np.random.standard_normal
    s = mx_kscale(K)[:, None]
    u = mx_kscale(H)[:, None]
    tab_words, tab_scales = pack_weight(n((K, T)) * s, "e4m3")
    w2_words, w2_scales = pack_weight(n((H, N)) / np.sqrt(H) / u, "e2m1")
    perm = np.random.permutation(S)
    sign = np.where(n(H) > 0, 1.0, -1.0)
    return {
        "tab_words": tab_words, "tab_scales": tab_scales,
        "offs": striped(np.random.permutation(T)[:S]),
        "pos1": striped(perm[:P]),
        "pos2": striped(perm[P:]),
        "w1": (n((K, H)) / np.sqrt(K) / s).astype(np.float32),
        "blank": (0.8 + 0.45 * n(H)).astype(np.float32),
        "temp": np.random.uniform(0.4, 1.6, H).astype(np.float32),
        "tilt": (sign * np.random.uniform(3.0, 7.0, H)).astype(np.float32),
        "skip": np.random.uniform(0.6, 1.6, H).astype(np.float32),
        "wgs": np.exp(0.3 * n((128, P))).astype(np.float32),
        "grain": (0.8 * n((H, S))).astype(np.float32),
        "gain": (np.random.uniform(0.6, 1.6, H) * u[:, 0]).astype(np.float32),
        "w2_words": w2_words, "w2_scales": w2_scales,
    }

def reference(tab_words, tab_scales, offs, pos1, pos2, w1, blank, temp, tilt, skip, wgs, grain, gain, w2_words, w2_scales):
    v = unpack_weight(tab_words, tab_scales, "e4m3")[:, unstriped(offs)]
    w2 = unpack_weight(w2_words, w2_scales, "e2m1")
    h = np.abs(mxq(f64(w1), 0, "e4m3").T @ v) - f64(blank)[:, None]
    top = h.max(axis=1)
    a = np.exp(f64(temp)[:, None] * (h[:, unstriped(pos1)] - top[:, None]))
    a = f64(tilt)[:, None] * a
    page = f64(skip)[:, None] * h
    page[:, unstriped(pos2)] = np.tile(f64(wgs), (H // 128, 1)) * a
    y = f64(gain)[:, None] * np.maximum(page, f64(grain))
    return w2.T @ mxq(y, 0, "e4m3")

@@ -1,0 +1,295 @@
+from contextlib import ExitStack
+
+import concourse.mybir as mybir
+
+T, S, LOOK, K, H, N = 2048, 1024, 512, 1024, 1024, 768
+FLOPS = 2 * K * H * S + 2 * H * N * S
+
+F32 = mybir.dt.float32
+BF16 = mybir.dt.bfloat16
+I32 = mybir.dt.int32
+U32 = mybir.dt.uint32
+U16 = mybir.dt.uint16
+U8 = mybir.dt.uint8
+FP8X4 = mybir.dt.float8_e4m3fn_x4
+FP4X4 = mybir.dt.float4_e2m1fn_x4
+ACT = mybir.ActivationFunctionType
+ALU = mybir.AluOpType
+
+P = 128
+PACK = 4
+PASS = P * PACK
+BANK = 512
+QUAD = 32
+PART = 256
+ROWSETS = H // P
+
+
+def tile_list_faded_ink_filler_kernel(
+    tc, tab_words, tab_scales, offs, pos1, pos2, w1, blank, temp, tilt, skip, wgs, grain, gain, w2_words, w2_scales, out
+):
+    nc = tc.nc
+    with ExitStack() as ctx:
+        lists = ctx.enter_context(tc.tile_pool(name="lists", bufs=1))
+        keep = ctx.enter_context(tc.tile_pool(name="keep", bufs=1))
+        ring = ctx.enter_context(tc.tile_pool(name="ring", bufs=2))
+        psum = ctx.enter_context(tc.psum_pool(name="psum", bufs=8))
+
+        offs_t = lists.tile([P, S // 16], U16, name="offs_t")
+        pos1_t = lists.tile([P, LOOK // 16], U16, name="pos1_t")
+        pos2_t = lists.tile([P, LOOK // 16], U16, name="pos2_t")
+
+        tab_s = keep.tile([P, T], U8, name="tab_s", align_bytes=64)
+        w2_s = keep.tile([P, 2, N], U8, name="w2_s", align_bytes=64)
+        nc.gpsimd.memset(tab_s[:].bitcast(I32), 0)
+        nc.vector.memset(w2_s[:].rearrange("p a n -> p (a n)").bitcast(I32), 0)
+
+        def load_w1(b, a):
+            raw = keep.tile([P, PACK, PASS], F32, name="w1_raw_%d_%d" % (b, a))
+            rows = w1[PASS * a : PASS * (a + 1), PASS * b : PASS * (b + 1)]
+            nc.sync.dma_start(out=raw[:], in_=rows.rearrange("(p j) c -> p j c", j=PACK))
+            return raw
+
+        def load_tab(a):
+            words = keep.tile([P, T], I32, name="tab_w_%d" % a)
+            nc.sync.dma_start(out=words[:], in_=tab_words[a].rearrange("p t i -> p (t i)").bitcast(I32))
+            return words
+
+        def load_grain(i):
+            b, t = divmod(i, PACK)
+            g = keep.tile([P, S], F32, name="grain_%d" % i)
+            nc.sync.dma_start(out=g[:], in_=grain.rearrange("(b p t) j -> b t p j", p=P, t=PACK)[b, t])
+            return g
+
+        def load_rowvec(vec, name):
+            v = keep.tile([P, ROWSETS], F32, name=name)
+            nc.gpsimd.dma_start(
+                out=v[:].rearrange("p (b t) -> p b t", t=PACK), in_=vec.rearrange("(b p t) -> p b t", p=P, t=PACK)
+            )
+            return v
+
+        nc.sync.dma_start(offs_t[:], offs)
+        for q in range(4):
+            nc.gpsimd.dma_start(
+                out=tab_s[QUAD * q : QUAD * q + 8, :].bitcast(I32), in_=tab_scales[:, 4 * q : 4 * q + 4, :].bitcast(I32)
+            )
+        w1_raw = {}
+        w1_raw[0, 0] = load_w1(0, 0)
+        tab_w = [load_tab(0), load_tab(1)]
+        w1_raw[0, 1] = load_w1(0, 1)
+        blank_t = load_rowvec(blank, "blank_t")
+        temp_t = load_rowvec(temp, "temp_t")
+        skip_t = load_rowvec(skip, "skip_t")
+        tilt_t = load_rowvec(tilt, "tilt_t")
+        gain_t = load_rowvec(gain, "gain_t")
+        nc.sync.dma_start(pos1_t[:], pos1)
+        nc.sync.dma_start(pos2_t[:], pos2)
+        wgs_t = keep.tile([P, PACK * LOOK], F32, name="wgs_t")
+        for q in (0, 2, 1, 3):
+            nc.sync.dma_start(
+                out=wgs_t[QUAD * q : QUAD * (q + 1), :], in_=wgs.rearrange("(q t) m -> q (t m)", t=PACK)
+            )
+        w1_raw[1, 0] = load_w1(1, 0)
+        grain_t = [load_grain(0)]
+        w1_raw[1, 1] = load_w1(1, 1)
+        grain_t.extend(load_grain(i) for i in range(1, PACK))
+        w2_w = keep.tile([P, 2, 2 * N], U8, name="w2_w", align_bytes=64)
+        nc.sync.dma_start(out=w2_w[:].bitcast(I32), in_=w2_words.rearrange("a p c -> p a c").bitcast(I32))
+        for q in range(4):
+            nc.sync.dma_start(
+                out=w2_s[QUAD * q : QUAD * q + 4, :, :].bitcast(I32),
+                in_=w2_scales[:, 4 * q : 4 * q + 4, :].rearrange("a r n -> r a n").bitcast(I32),
+            )
+        grain_t.extend(load_grain(i) for i in range(PACK, ROWSETS))
+
+        neg_temp = keep.tile([P, ROWSETS], F32, name="neg_temp")
+        nc.gpsimd.tensor_scalar(neg_temp[:], temp_t[:], -1.0, 0.0, ALU.mult, ALU.add)
+
+        def scalar_copy(dst, src):
+            nc.scalar.activation(out=dst, in_=src, func=ACT.Copy)
+
+        w1_codes = {}
+        w1_scales = {}
+
+        def weave_w1(engine_copy, b, a, pair):
+            woven = ring.tile([P, 2 * PASS], BF16, name="w1_woven", bufs=4, align_bytes=64)
+            engine_copy(
+                woven[:].rearrange("p (t m j) -> p m j t", t=2, j=PACK),
+                w1_raw[b, a][:].rearrange("p j (m t) -> p m j t", t=PACK)[:, :, :, 2 * pair : 2 * pair + 2],
+            )
+            return woven
+
+        def quantize_w1(b, a, pair, woven):
+            codes = keep.tile([P, 2 * P], U32, name="w1_codes_%d_%d_%d" % (b, a, pair), align_bytes=64)
+            scales = keep.tile([P, 2 * P], U8, name="w1_scales_%d_%d_%d" % (b, a, pair), align_bytes=64)
+            nc.vector.quantize_mx(out=codes[:].bitcast(FP8X4), scales=scales[:], in_=woven[:])
+            w1_codes[b, a, pair] = codes
+            w1_scales[b, a, pair] = scales
+
+        def gather_words(a, half):
+            g = keep.tile([P, BANK], U32, name="v_words_%d_%d" % (a, half), align_bytes=64)
+            cols = slice(half * BANK // 16, (half + 1) * BANK // 16)
+            nc.vector.tensor_copy(g[:], tab_w[a][:].bitcast(U32).indirect(offs_t[:, cols]))
+            return g
+
+        v_scales = keep.tile([P, S], U8, name="v_scales", align_bytes=64)
+        nc.vector.tensor_copy(v_scales[:], tab_s[:].indirect(offs_t[:]))
+        first = [weave_w1(scalar_copy, 0, 0, pair) for pair in range(2)]
+        v_words = {}
+        for half in range(2):
+            v_words[0, half] = gather_words(0, half)
+        for pair in range(2):
+            quantize_w1(0, 0, pair, first[pair])
+        for half in range(2):
+            v_words[1, half] = gather_words(1, half)
+        woven_a = weave_w1(nc.vector.tensor_copy, 0, 1, 0)
+        woven_b = weave_w1(scalar_copy, 0, 1, 1)
+        quantize_w1(0, 1, 0, woven_a)
+        quantize_w1(0, 1, 1, woven_b)
+
+        tilted = []
+        for i in range(ROWSETS):
+            t = i % PACK
+            tw = keep.tile([P, LOOK], F32, name="tilted_%d" % i)
+            nc.gpsimd.tensor_scalar(
+                tw[:], wgs_t[:, LOOK * t : LOOK * (t + 1)], tilt_t[:, i : i + 1], 0.0, ALU.mult, ALU.add
+            )
+            tilted.append(tw)
+
+        top = keep.tile([P, ROWSETS], F32, name="top")
+        look_bias = keep.tile([P, ROWSETS], F32, name="look_bias")
+        h_t, look_t, page_t, best_t = {}, {}, {}, {}
+        parts = S // PART
+        y_rows = [keep.tile([P, parts, PACK, PART], BF16, name="y_rows_%d" % b) for b in range(2)]
+        y_codes = [keep.tile([P, S], U32, name="y_codes_%d" % b, align_bytes=64) for b in range(2)]
+        y_scales = [keep.tile([P, S], U8, name="y_scales_%d" % b, align_bytes=64) for b in range(2)]
+
+        def features(i):
+            b, t = divmod(i, PACK)
+            pair, cols = t // 2, slice(P * (t % 2), P * (t % 2 + 1))
+            size = ring.tile([P, S], F32, name="size")
+            for half in range(2):
+                acc = psum.tile([P, BANK], F32, name="acc")
+                for a in range(2):
+                    nc.tensor.matmul_mx(
+                        out=acc[:],
+                        lhsT=w1_codes[b, a, pair][:, cols].bitcast(FP8X4),
+                        lhsT_scale=w1_scales[b, a, pair][:, cols],
+                        rhs=v_words[a, half][:].bitcast(FP8X4),
+                        rhs_scale=v_scales[4 * a :, BANK * half : BANK * (half + 1)],
+                        start=(a == 0),
+                        stop=(a == 1),
+                    )
+                nc.scalar.activation(out=size[:, BANK * half : BANK * (half + 1)], in_=acc[:], func=ACT.Abs)
+            h = ring.tile([P, S], F32, name="h", bufs=3)
+            nc.vector.tensor_scalar(
+                h[:], size[:], blank_t[:, i : i + 1], None, ALU.subtract, ALU.max, accum_out=top[:, i : i + 1]
+            )
+            h_t[i] = h
+
+        def look_and_page(i):
+            col = slice(i, i + 1)
+            nc.scalar.activation(out=look_bias[:, col], in_=top[:, col], func=ACT.Copy, scale=neg_temp[:, col])
+            page = ring.tile([P, S], F32, name="page", bufs=3)
+            nc.scalar.activation(out=page[:], in_=h_t[i][:], func=ACT.Copy, scale=skip_t[:, col])
+            look = ring.tile([P, LOOK], F32, name="look", bufs=3)
+            nc.scalar.activation(
+                out=look[:], in_=h_t[i][:].indirect(pos1_t[:]), func=ACT.Exp, bias=look_bias[:, col], scale=temp_t[:, col]
+            )
+            look_t[i], page_t[i] = look, page
+
+        def write_page(i):
+            nc.vector.tensor_tensor(page_t[i][:].indirect(pos2_t[:]), look_t[i][:], tilted[i][:], ALU.mult)
+
+        def meet_grain(i, cols):
+            if i not in best_t:
+                tag = "best" if i < ROWSETS - 2 else "best_%d" % i
+                best_t[i] = ring.tile([P, S], F32, name=tag, bufs=1)
+            nc.vector.tensor_tensor(best_t[i][:, cols], page_t[i][:, cols], grain_t[i][:, cols], ALU.max)
+
+        def apply_gain(i, lo, hi):
+            b, t = divmod(i, PACK)
+            nc.scalar.activation(
+                out=y_rows[b][:, lo:hi, t, :],
+                in_=best_t[i][:, PART * lo : PART * hi].rearrange("p (q c) -> p q c", c=PART),
+                func=ACT.Copy,
+                scale=gain_t[:, i : i + 1],
+            )
+
+        def weave_y(engine_copy, b, q):
+            woven = ring.tile([P, PACK * PART], BF16, name="y_woven", bufs=4, align_bytes=64)
+            engine_copy(
+                woven[:].rearrange("p (c i t) -> p c t i", i=4, t=PACK),
+                y_rows[b][:, q, :, :].rearrange("p t (c i) -> p c t i", i=4),
+            )
+            return woven
+
+        def quantize_y(b, q, woven):
+            cols = slice(PART * q, PART * (q + 1))
+            nc.vector.quantize_mx(out=y_codes[b][:, cols].bitcast(FP8X4), scales=y_scales[b][:, cols], in_=woven[:])
+
+        features(0)
+        features(1)
+        look_and_page(0)
+        write_page(0)
+        last = ROWSETS - 1
+        for r in range(ROWSETS):
+            if r + 2 < ROWSETS:
+                features(r + 2)
+            if r + 1 < ROWSETS:
+                look_and_page(r + 1)
+                write_page(r + 1)
+            if r >= 1:
+                apply_gain(r - 1, 0, parts)
+            if r < last:
+                meet_grain(r, slice(0, S))
+            if r == 0:
+                for a in range(2):
+                    quantize_w1(1, a, 0, weave_w1(scalar_copy, 1, a, 0))
+            if r in (1, 2):
+                quantize_w1(1, r - 1, 1, weave_w1(scalar_copy, 1, r - 1, 1))
+            if r == 4:
+                for q in (0, 1):
+                    quantize_y(0, q, weave_y(nc.scalar.copy, 0, q))
+            if r in (5, 6):
+                quantize_y(0, r - 3, weave_y(nc.scalar.copy, 0, r - 3))
+
+        groups = [(half, n) for half in range(2) for n in range(N // P)]
+        sums = {}
+
+        def read_out(g, b):
+            half, n = groups[g]
+            if b == 0:
+                sums[g] = psum.tile([P, BANK], F32, name="acc")
+            cols = slice(BANK * half, BANK * (half + 1))
+            nc.tensor.matmul_mx(
+                out=sums[g][:],
+                lhsT=w2_w[:, b, 2 * P * n : 2 * P * (n + 1)].bitcast(FP4X4),
+                lhsT_scale=w2_s[:, b, P * n : P * (n + 1)],
+                rhs=y_codes[b][:, cols].bitcast(FP8X4),
+                rhs_scale=y_scales[b][:, cols],
+                start=(b == 0),
+                stop=(b == 1),
+            )
+
+        def store(g, engine_copy):
+            half, n = groups[g]
+            staged = ring.tile([P, BANK], F32, name="staged", bufs=6)
+            engine_copy(staged[:], sums[g][:])
+            nc.sync.dma_start(out=out[P * n : P * (n + 1), BANK * half : BANK * (half + 1)], in_=staged[:])
+
+        for g in range(8):
+            read_out(g, 0)
+        for half in range(2):
+            quarters = (2 * half, 2 * half + 1)
+            for q in quarters:
+                meet_grain(last, slice(PART * q, PART * (q + 1)))
+                apply_gain(last, q, q + 1)
+            woven = [weave_y(nc.vector.tensor_copy, 1, q) for q in quarters]
+            for q, w in zip(quarters, woven):
+                quantize_y(1, q, w)
+        for g in range(len(groups)):
+            if g >= 8:
+                read_out(g, 0)
+            read_out(g, 1)
+            store(g, nc.vector.tensor_copy if g >= 6 and g % 2 == 0 else nc.scalar.copy)

@@ -23,6 +23,7 @@ BANK = 512
 QUAD = 32
 PART = 256
 ROWSETS = H // P
+SIZE_SLOT = (0, 1, 2, 0, 1, 0, 2, 1)
 
 
 def tile_list_faded_ink_filler_kernel(
@@ -33,7 +34,7 @@ def tile_list_faded_ink_filler_kernel(
         lists = ctx.enter_context(tc.tile_pool(name="lists", bufs=1))
         keep = ctx.enter_context(tc.tile_pool(name="keep", bufs=1))
         ring = ctx.enter_context(tc.tile_pool(name="ring", bufs=2))
-        psum = ctx.enter_context(tc.psum_pool(name="psum", bufs=8))
+        psum = ctx.enter_context(tc.psum_pool(name="psum", bufs=4))
 
         offs_t = lists.tile([P, S // 16], U16, name="offs_t")
         pos1_t = lists.tile([P, LOOK // 16], U16, name="pos1_t")
@@ -41,7 +42,8 @@ def tile_list_faded_ink_filler_kernel(
 
         tab_s = keep.tile([P, T], U8, name="tab_s", align_bytes=64)
         w2_s = keep.tile([P, 2, N], U8, name="w2_s", align_bytes=64)
-        nc.gpsimd.memset(tab_s[:].bitcast(I32), 0)
+        tab_s_rows = keep.tile([P, T // 4], I32, name="tab_s_rows")
+        nc.vector.memset(tab_s[:].bitcast(I32), 0)
         nc.vector.memset(w2_s[:].rearrange("p a n -> p (a n)").bitcast(I32), 0)
 
         def load_w1(b, a):
@@ -70,12 +72,12 @@ def tile_list_faded_ink_filler_kernel(
 
         nc.sync.dma_start(offs_t[:], offs)
         for q in range(4):
-            nc.gpsimd.dma_start(
-                out=tab_s[QUAD * q : QUAD * q + 8, :].bitcast(I32), in_=tab_scales[:, 4 * q : 4 * q + 4, :].bitcast(I32)
+            nc.sync.dma_start(
+                out=tab_s_rows[QUAD * q : QUAD * q + 8, :], in_=tab_scales[:, 4 * q : 4 * q + 4, :].bitcast(I32)
             )
+        tab_w = [load_tab(0), load_tab(1)]
         w1_raw = {}
         w1_raw[0, 0] = load_w1(0, 0)
-        tab_w = [load_tab(0), load_tab(1)]
         w1_raw[0, 1] = load_w1(0, 1)
         blank_t = load_rowvec(blank, "blank_t")
         temp_t = load_rowvec(temp, "temp_t")
@@ -84,14 +86,18 @@ def tile_list_faded_ink_filler_kernel(
         gain_t = load_rowvec(gain, "gain_t")
         nc.sync.dma_start(pos1_t[:], pos1)
         nc.sync.dma_start(pos2_t[:], pos2)
-        wgs_t = keep.tile([P, PACK * LOOK], F32, name="wgs_t")
-        for q in (0, 2, 1, 3):
-            nc.sync.dma_start(
-                out=wgs_t[QUAD * q : QUAD * (q + 1), :], in_=wgs.rearrange("(q t) m -> q (t m)", t=PACK)
-            )
+        def load_wgs(pair):
+            dealt = keep.tile([P, 2 * LOOK], F32, name="wgs_%d" % pair)
+            rows = wgs.rearrange("(q t) m -> q (t m)", t=PACK)[:, 2 * LOOK * pair : 2 * LOOK * (pair + 1)]
+            for q in (0, 2, 1, 3):
+                nc.sync.dma_start(out=dealt[QUAD * q : QUAD * (q + 1), :], in_=rows)
+            return dealt
+
+        wgs_t = [load_wgs(0)]
         w1_raw[1, 0] = load_w1(1, 0)
-        grain_t = [load_grain(0)]
+        wgs_t.append(load_wgs(1))
         w1_raw[1, 1] = load_w1(1, 1)
+        grain_t = [load_grain(0)]
         grain_t.extend(load_grain(i) for i in range(1, PACK))
         w2_w = keep.tile([P, 2, 2 * N], U8, name="w2_w", align_bytes=64)
         nc.sync.dma_start(out=w2_w[:].bitcast(I32), in_=w2_words.rearrange("a p c -> p a c").bitcast(I32))
@@ -111,10 +117,11 @@ def tile_list_faded_ink_filler_kernel(
         w1_codes = {}
         w1_scales = {}
 
-        def weave_w1(engine_copy, b, a, pair):
-            woven = ring.tile([P, 2 * PASS], BF16, name="w1_woven", bufs=4, align_bytes=64)
+        def weave_w1(engine_copy, b, a, pair, woven=None):
+            if woven is None:
+                woven = ring.tile([P, 2 * PASS], BF16, name="w1_woven", bufs=4, align_bytes=64)[:]
             engine_copy(
-                woven[:].rearrange("p (t m j) -> p m j t", t=2, j=PACK),
+                woven.rearrange("p (t m j) -> p m j t", t=2, j=PACK),
                 w1_raw[b, a][:].rearrange("p j (m t) -> p m j t", t=PACK)[:, :, :, 2 * pair : 2 * pair + 2],
             )
             return woven
@@ -122,7 +129,7 @@ def tile_list_faded_ink_filler_kernel(
         def quantize_w1(b, a, pair, woven):
             codes = keep.tile([P, 2 * P], U32, name="w1_codes_%d_%d_%d" % (b, a, pair), align_bytes=64)
             scales = keep.tile([P, 2 * P], U8, name="w1_scales_%d_%d_%d" % (b, a, pair), align_bytes=64)
-            nc.vector.quantize_mx(out=codes[:].bitcast(FP8X4), scales=scales[:], in_=woven[:])
+            nc.vector.quantize_mx(out=codes[:].bitcast(FP8X4), scales=scales[:], in_=woven)
             w1_codes[b, a, pair] = codes
             w1_scales[b, a, pair] = scales
 
@@ -132,44 +139,60 @@ def tile_list_faded_ink_filler_kernel(
             nc.vector.tensor_copy(g[:], tab_w[a][:].bitcast(U32).indirect(offs_t[:, cols]))
             return g
 
+        for q in range(4):
+            rows = slice(QUAD * q, QUAD * q + 8)
+            nc.vector.tensor_copy(tab_s[rows, :].bitcast(I32), tab_s_rows[rows, :])
         v_scales = keep.tile([P, S], U8, name="v_scales", align_bytes=64)
         nc.vector.tensor_copy(v_scales[:], tab_s[:].indirect(offs_t[:]))
-        first = [weave_w1(scalar_copy, 0, 0, pair) for pair in range(2)]
         v_words = {}
-        for half in range(2):
-            v_words[0, half] = gather_words(0, half)
-        for pair in range(2):
-            quantize_w1(0, 0, pair, first[pair])
-        for half in range(2):
-            v_words[1, half] = gather_words(1, half)
-        woven_a = weave_w1(nc.vector.tensor_copy, 0, 1, 0)
-        woven_b = weave_w1(scalar_copy, 0, 1, 1)
-        quantize_w1(0, 1, 0, woven_a)
-        quantize_w1(0, 1, 1, woven_b)
+        for a in range(2):
+            for half in range(2):
+                v_words[a, half] = gather_words(a, half)
+        quantize_w1(0, 0, 0, weave_w1(scalar_copy, 0, 0, 0))
+        quantize_w1(0, 1, 0, weave_w1(nc.vector.tensor_copy, 0, 1, 0))
+        later_pair = [weave_w1(scalar_copy, 0, a, 1) for a in range(2)]
 
-        tilted = []
-        for i in range(ROWSETS):
+        tilted = {}
+        tilted_first = keep.tile([P, LOOK], F32, name="tilted_first")
+        best_slot = keep.tile([P, S], F32, name="best")
+
+        def tilt_weights(i):
             t = i % PACK
-            tw = keep.tile([P, LOOK], F32, name="tilted_%d" % i)
+            if i in (0, 2):
+                tw = tilted_first[:]
+            elif i == 1:
+                tw = best_slot[:, 0:LOOK]
+            else:
+                tw = grain_t[i - 3][:, 0:LOOK]
             nc.gpsimd.tensor_scalar(
-                tw[:], wgs_t[:, LOOK * t : LOOK * (t + 1)], tilt_t[:, i : i + 1], 0.0, ALU.mult, ALU.add
+                tw, wgs_t[t // 2][:, LOOK * (t % 2) : LOOK * (t % 2 + 1)], tilt_t[:, i : i + 1], 0.0, ALU.mult, ALU.add
             )
-            tilted.append(tw)
+            tilted[i] = tw
 
         top = keep.tile([P, ROWSETS], F32, name="top")
         look_bias = keep.tile([P, ROWSETS], F32, name="look_bias")
-        h_t, look_t, page_t, best_t = {}, {}, {}, {}
+        h_t, look_t, page_t = {}, {}, {}
+        size_slots = [keep.tile([P, S], F32, name="size_%d" % k, align_bytes=64) for k in range(3)]
+        h_slots = [keep.tile([P, S], F32, name="h_%d" % k) for k in range(3)]
+        best_t = [best_slot if i < ROWSETS - 2 else grain_t[i - 1] for i in range(ROWSETS)]
         parts = S // PART
         y_rows = [keep.tile([P, parts, PACK, PART], BF16, name="y_rows_%d" % b) for b in range(2)]
-        y_codes = [keep.tile([P, S], U32, name="y_codes_%d" % b, align_bytes=64) for b in range(2)]
-        y_scales = [keep.tile([P, S], U8, name="y_scales_%d" % b, align_bytes=64) for b in range(2)]
+        spans = ((0, 1), (1, 2), (2, 4))
+        y_codes, y_scales = {}, {}
+        for b in range(2):
+            for k, (lo, hi) in enumerate(spans):
+                width = PART * (hi - lo)
+                if (b, k) != (1, 0):
+                    y_codes[b, k] = keep.tile([P, width], U32, name="y_codes_%d_%d" % (b, k), align_bytes=64)[:]
+                y_scales[b, k] = keep.tile([P, width], U8, name="y_scales_%d_%d" % (b, k), align_bytes=64)[:]
+        y_codes[1, 0] = y_codes[0, 2][:, 0:PART]
 
         def features(i):
             b, t = divmod(i, PACK)
             pair, cols = t // 2, slice(P * (t % 2), P * (t % 2 + 1))
-            size = ring.tile([P, S], F32, name="size")
+            size = size_slots[SIZE_SLOT[i]]
             for half in range(2):
-                acc = psum.tile([P, BANK], F32, name="acc")
+                acc = psum.tile([P, BANK], F32, name="acc", tag="banks_1")
                 for a in range(2):
                     nc.tensor.matmul_mx(
                         out=acc[:],
@@ -181,7 +204,7 @@ def tile_list_faded_ink_filler_kernel(
                         stop=(a == 1),
                     )
                 nc.scalar.activation(out=size[:, BANK * half : BANK * (half + 1)], in_=acc[:], func=ACT.Abs)
-            h = ring.tile([P, S], F32, name="h", bufs=3)
+            h = h_slots[i % 3]
             nc.vector.tensor_scalar(
                 h[:], size[:], blank_t[:, i : i + 1], None, ALU.subtract, ALU.max, accum_out=top[:, i : i + 1]
             )
@@ -191,20 +214,21 @@ def tile_list_faded_ink_filler_kernel(
             col = slice(i, i + 1)
             nc.scalar.activation(out=look_bias[:, col], in_=top[:, col], func=ACT.Copy, scale=neg_temp[:, col])
             page = ring.tile([P, S], F32, name="page", bufs=3)
-            nc.scalar.activation(out=page[:], in_=h_t[i][:], func=ACT.Copy, scale=skip_t[:, col])
-            look = ring.tile([P, LOOK], F32, name="look", bufs=3)
+            if i == 0:
+                nc.vector.tensor_scalar(page[:], h_t[i][:], skip_t[:, col], None, ALU.mult)
+            else:
+                nc.scalar.activation(out=page[:], in_=h_t[i][:], func=ACT.Copy, scale=skip_t[:, col])
+            look = h_slots[(i - 1) % 3][:, 0:LOOK]
             nc.scalar.activation(
-                out=look[:], in_=h_t[i][:].indirect(pos1_t[:]), func=ACT.Exp, bias=look_bias[:, col], scale=temp_t[:, col]
+                out=look, in_=h_t[i][:].indirect(pos1_t[:]), func=ACT.Exp, bias=look_bias[:, col], scale=temp_t[:, col]
             )
             look_t[i], page_t[i] = look, page
 
         def write_page(i):
-            nc.vector.tensor_tensor(page_t[i][:].indirect(pos2_t[:]), look_t[i][:], tilted[i][:], ALU.mult)
+            tilt_weights(i)
+            nc.vector.tensor_tensor(page_t[i][:].indirect(pos2_t[:]), look_t[i], tilted[i], ALU.mult)
 
         def meet_grain(i, cols):
-            if i not in best_t:
-                tag = "best" if i < ROWSETS - 2 else "best_%d" % i
-                best_t[i] = ring.tile([P, S], F32, name=tag, bufs=1)
             nc.vector.tensor_tensor(best_t[i][:, cols], page_t[i][:, cols], grain_t[i][:, cols], ALU.max)
 
         def apply_gain(i, lo, hi):
@@ -216,80 +240,107 @@ def tile_list_faded_ink_filler_kernel(
                 scale=gain_t[:, i : i + 1],
             )
 
-        def weave_y(engine_copy, b, q):
-            woven = ring.tile([P, PACK * PART], BF16, name="y_woven", bufs=4, align_bytes=64)
+        def weave_y(engine_copy, b, q, woven):
             engine_copy(
-                woven[:].rearrange("p (c i t) -> p c t i", i=4, t=PACK),
+                woven.rearrange("p (c i t) -> p c t i", i=4, t=PACK),
                 y_rows[b][:, q, :, :].rearrange("p t (c i) -> p c t i", i=4),
             )
-            return woven
 
-        def quantize_y(b, q, woven):
-            cols = slice(PART * q, PART * (q + 1))
-            nc.vector.quantize_mx(out=y_codes[b][:, cols].bitcast(FP8X4), scales=y_scales[b][:, cols], in_=woven[:])
+        def woven_tile(name, quarters):
+            return keep.tile([P, quarters * PACK * PART], BF16, name=name, align_bytes=64)
+
+        def quantize_y(b, k, woven):
+            nc.vector.quantize_mx(out=y_codes[b, k].bitcast(FP8X4), scales=y_scales[b, k], in_=woven)
+
+        quarter = PACK * PART
+        woven_q = [woven_tile("y_woven_q%d" % q, 1) for q in range(2)]
+        woven_half = [woven_tile("y_woven_half%d" % b, 2) for b in range(2)]
 
         features(0)
         features(1)
+        for a in range(2):
+            quantize_w1(0, a, 1, later_pair[a])
         look_and_page(0)
         write_page(0)
         last = ROWSETS - 1
-        for r in range(ROWSETS):
+        for r in range(last):
             if r + 2 < ROWSETS:
                 features(r + 2)
-            if r + 1 < ROWSETS:
-                look_and_page(r + 1)
+            look_and_page(r + 1)
+            if r + 1 < last:
                 write_page(r + 1)
-            if r >= 1:
-                apply_gain(r - 1, 0, parts)
-            if r < last:
-                meet_grain(r, slice(0, S))
+            if r in (0, 1):
+                late = size_slots[r + 1][:].bitcast(BF16).rearrange("p (a c) -> p a c", a=2)
             if r == 0:
                 for a in range(2):
-                    quantize_w1(1, a, 0, weave_w1(scalar_copy, 1, a, 0))
+                    quantize_w1(1, a, 0, weave_w1(scalar_copy, 1, a, 0, late[:, a, :]))
             if r in (1, 2):
-                quantize_w1(1, r - 1, 1, weave_w1(scalar_copy, 1, r - 1, 1))
+                quantize_w1(1, r - 1, 1, weave_w1(scalar_copy, 1, r - 1, 1, late[:, r - 1, :]))
+            if r == 5:
+                weave_y(nc.scalar.copy, 0, 1, woven_q[1][:])
+                quantize_y(0, 1, woven_q[1][:])
+            if r == 6:
+                for q in (2, 3):
+                    weave_y(nc.scalar.copy, 0, q, woven_half[0][:, quarter * (q - 2) : quarter * (q - 1)])
+            if r >= 1:
+                apply_gain(r - 1, 0, parts)
+            meet_grain(r, slice(0, S))
             if r == 4:
-                for q in (0, 1):
-                    quantize_y(0, q, weave_y(nc.scalar.copy, 0, q))
-            if r in (5, 6):
-                quantize_y(0, r - 3, weave_y(nc.scalar.copy, 0, r - 3))
+                weave_y(nc.scalar.copy, 0, 0, woven_q[0][:])
+                quantize_y(0, 0, woven_q[0][:])
+        write_page(last)
+        apply_gain(last - 1, 0, parts)
 
-        groups = [(half, n) for half in range(2) for n in range(N // P)]
+        banks = [(k, n, 2) for k in range(2) for n in range(0, N // P, 2)] + [(2, n, 1) for n in range(N // P)]
         sums = {}
 
         def read_out(g, b):
-            half, n = groups[g]
+            k, n0, count = banks[g]
             if b == 0:
-                sums[g] = psum.tile([P, BANK], F32, name="acc")
-            cols = slice(BANK * half, BANK * (half + 1))
-            nc.tensor.matmul_mx(
-                out=sums[g][:],
-                lhsT=w2_w[:, b, 2 * P * n : 2 * P * (n + 1)].bitcast(FP4X4),
-                lhsT_scale=w2_s[:, b, P * n : P * (n + 1)],
-                rhs=y_codes[b][:, cols].bitcast(FP8X4),
-                rhs_scale=y_scales[b][:, cols],
-                start=(b == 0),
-                stop=(b == 1),
-            )
+                sums[g] = psum.tile([P, BANK], F32, name="sums", tag="banks_%d" % (g // 4 % 2))
+            width = BANK // count
+            for m in range(count):
+                n = n0 + m
+                nc.tensor.matmul_mx(
+                    out=sums[g][:, width * m : width * (m + 1)],
+                    lhsT=w2_w[:, b, 2 * P * n : 2 * P * (n + 1)].bitcast(FP4X4),
+                    lhsT_scale=w2_s[:, b, P * n : P * (n + 1)],
+                    rhs=y_codes[b, k].bitcast(FP8X4),
+                    rhs_scale=y_scales[b, k],
+                    start=(b == 0 and m == 0),
+                    stop=(b == 1 and m == count - 1),
+                )
 
         def store(g, engine_copy):
-            half, n = groups[g]
-            staged = ring.tile([P, BANK], F32, name="staged", bufs=6)
+            k, n0, count = banks[g]
+            staged = ring.tile([P, BANK], F32, name="staged", bufs=12)
             engine_copy(staged[:], sums[g][:])
-            nc.sync.dma_start(out=out[P * n : P * (n + 1), BANK * half : BANK * (half + 1)], in_=staged[:])
+            lo, hi = spans[k]
+            nc.sync.dma_start(
+                out=out[P * n0 : P * (n0 + count), PART * lo : PART * hi].rearrange("(m p) c -> p m c", p=P),
+                in_=staged[:].rearrange("p (m c) -> p m c", m=count),
+            )
 
-        for g in range(8):
+        for g in range(6):
             read_out(g, 0)
-        for half in range(2):
-            quarters = (2 * half, 2 * half + 1)
-            for q in quarters:
-                meet_grain(last, slice(PART * q, PART * (q + 1)))
-                apply_gain(last, q, q + 1)
-            woven = [weave_y(nc.vector.tensor_copy, 1, q) for q in quarters]
-            for q, w in zip(quarters, woven):
-                quantize_y(1, q, w)
-        for g in range(len(groups)):
-            if g >= 8:
+        for q in range(parts):
+            meet_grain(last, slice(PART * q, PART * (q + 1)))
+            apply_gain(last, q, q + 1)
+        weave_y(nc.vector.tensor_copy, 1, 0, woven_half[1][:, 0:quarter])
+        quantize_y(1, 0, woven_half[1][:, 0:quarter])
+        weave_y(nc.scalar.copy, 1, 1, woven_q[1][:])
+        for g in range(3):
+            read_out(g, 1)
+            store(g, nc.scalar.copy)
+        nc.vector.tensor_copy(
+            woven_half[1][:].rearrange("p (q c i t) -> p q c t i", q=2, i=4, t=PACK),
+            y_rows[1][:, 2:4, :, :].rearrange("p q t (c i) -> p q c t i", i=4),
+        )
+        quantize_y(1, 1, woven_q[1][:])
+        quantize_y(0, 2, woven_half[0][:])
+        quantize_y(1, 2, woven_half[1][:])
+        for g in range(3, len(banks)):
+            if g >= 6:
                 read_out(g, 0)
             read_out(g, 1)
-            store(g, nc.vector.tensor_copy if g >= 6 and g % 2 == 0 else nc.scalar.copy)
+            store(g, nc.vector.tensor_copy if g in (6, 7, 9, 11) else nc.scalar.copy)

from contextlib import ExitStack

import concourse.mybir as mybir

T, S, LOOK, K, H, N = 2048, 1024, 512, 1024, 1024, 768
FLOPS = 2 * K * H * S + 2 * H * N * S

F32 = mybir.dt.float32
BF16 = mybir.dt.bfloat16
I32 = mybir.dt.int32
U32 = mybir.dt.uint32
U16 = mybir.dt.uint16
U8 = mybir.dt.uint8
FP8X4 = mybir.dt.float8_e4m3fn_x4
FP4X4 = mybir.dt.float4_e2m1fn_x4
ACT = mybir.ActivationFunctionType
ALU = mybir.AluOpType

P = 128
PACK = 4
PASS = P * PACK
BANK = 512
QUAD = 32
PART = 256
ROWSETS = H // P
SIZE_SLOT = (0, 1, 2, 0, 1, 0, 2, 1)


def tile_list_faded_ink_filler_kernel(
    tc, tab_words, tab_scales, offs, pos1, pos2, w1, blank, temp, tilt, skip, wgs, grain, gain, w2_words, w2_scales, out
):
    nc = tc.nc
    with ExitStack() as ctx:
        lists = ctx.enter_context(tc.tile_pool(name="lists", bufs=1))
        keep = ctx.enter_context(tc.tile_pool(name="keep", bufs=1))
        ring = ctx.enter_context(tc.tile_pool(name="ring", bufs=2))
        psum = ctx.enter_context(tc.psum_pool(name="psum", bufs=4))

        offs_t = lists.tile([P, S // 16], U16, name="offs_t")
        pos1_t = lists.tile([P, LOOK // 16], U16, name="pos1_t")
        pos2_t = lists.tile([P, LOOK // 16], U16, name="pos2_t")

        tab_s = keep.tile([P, T], U8, name="tab_s", align_bytes=64)
        w2_s = keep.tile([P, 2, N], U8, name="w2_s", align_bytes=64)
        tab_s_rows = keep.tile([P, T // 4], I32, name="tab_s_rows")
        nc.vector.memset(tab_s[:].bitcast(I32), 0)
        nc.vector.memset(w2_s[:].rearrange("p a n -> p (a n)").bitcast(I32), 0)

        def load_w1(b, a):
            raw = keep.tile([P, PACK, PASS], F32, name="w1_raw_%d_%d" % (b, a))
            rows = w1[PASS * a : PASS * (a + 1), PASS * b : PASS * (b + 1)]
            nc.sync.dma_start(out=raw[:], in_=rows.rearrange("(p j) c -> p j c", j=PACK))
            return raw

        def load_tab(a):
            words = keep.tile([P, T], I32, name="tab_w_%d" % a)
            nc.sync.dma_start(out=words[:], in_=tab_words[a].rearrange("p t i -> p (t i)").bitcast(I32))
            return words

        def load_grain(i):
            b, t = divmod(i, PACK)
            g = keep.tile([P, S], F32, name="grain_%d" % i)
            nc.sync.dma_start(out=g[:], in_=grain.rearrange("(b p t) j -> b t p j", p=P, t=PACK)[b, t])
            return g

        def load_rowvec(vec, name):
            v = keep.tile([P, ROWSETS], F32, name=name)
            nc.gpsimd.dma_start(
                out=v[:].rearrange("p (b t) -> p b t", t=PACK), in_=vec.rearrange("(b p t) -> p b t", p=P, t=PACK)
            )
            return v

        nc.sync.dma_start(offs_t[:], offs)
        for q in range(4):
            nc.sync.dma_start(
                out=tab_s_rows[QUAD * q : QUAD * q + 8, :], in_=tab_scales[:, 4 * q : 4 * q + 4, :].bitcast(I32)
            )
        tab_w = [load_tab(0), load_tab(1)]
        w1_raw = {}
        w1_raw[0, 0] = load_w1(0, 0)
        w1_raw[0, 1] = load_w1(0, 1)
        blank_t = load_rowvec(blank, "blank_t")
        temp_t = load_rowvec(temp, "temp_t")
        skip_t = load_rowvec(skip, "skip_t")
        tilt_t = load_rowvec(tilt, "tilt_t")
        gain_t = load_rowvec(gain, "gain_t")
        nc.sync.dma_start(pos1_t[:], pos1)
        nc.sync.dma_start(pos2_t[:], pos2)
        def load_wgs(pair):
            dealt = keep.tile([P, 2 * LOOK], F32, name="wgs_%d" % pair)
            rows = wgs.rearrange("(q t) m -> q (t m)", t=PACK)[:, 2 * LOOK * pair : 2 * LOOK * (pair + 1)]
            for q in (0, 2, 1, 3):
                nc.sync.dma_start(out=dealt[QUAD * q : QUAD * (q + 1), :], in_=rows)
            return dealt

        wgs_t = [load_wgs(0)]
        w1_raw[1, 0] = load_w1(1, 0)
        wgs_t.append(load_wgs(1))
        w1_raw[1, 1] = load_w1(1, 1)
        grain_t = [load_grain(0)]
        grain_t.extend(load_grain(i) for i in range(1, PACK))
        w2_w = keep.tile([P, 2, 2 * N], U8, name="w2_w", align_bytes=64)
        nc.sync.dma_start(out=w2_w[:].bitcast(I32), in_=w2_words.rearrange("a p c -> p a c").bitcast(I32))
        for q in range(4):
            nc.sync.dma_start(
                out=w2_s[QUAD * q : QUAD * q + 4, :, :].bitcast(I32),
                in_=w2_scales[:, 4 * q : 4 * q + 4, :].rearrange("a r n -> r a n").bitcast(I32),
            )
        grain_t.extend(load_grain(i) for i in range(PACK, ROWSETS))

        neg_temp = keep.tile([P, ROWSETS], F32, name="neg_temp")
        nc.gpsimd.tensor_scalar(neg_temp[:], temp_t[:], -1.0, 0.0, ALU.mult, ALU.add)

        def scalar_copy(dst, src):
            nc.scalar.activation(out=dst, in_=src, func=ACT.Copy)

        w1_codes = {}
        w1_scales = {}

        def weave_w1(engine_copy, b, a, pair, woven=None):
            if woven is None:
                woven = ring.tile([P, 2 * PASS], BF16, name="w1_woven", bufs=4, align_bytes=64)[:]
            engine_copy(
                woven.rearrange("p (t m j) -> p m j t", t=2, j=PACK),
                w1_raw[b, a][:].rearrange("p j (m t) -> p m j t", t=PACK)[:, :, :, 2 * pair : 2 * pair + 2],
            )
            return woven

        def quantize_w1(b, a, pair, woven):
            codes = keep.tile([P, 2 * P], U32, name="w1_codes_%d_%d_%d" % (b, a, pair), align_bytes=64)
            scales = keep.tile([P, 2 * P], U8, name="w1_scales_%d_%d_%d" % (b, a, pair), align_bytes=64)
            nc.vector.quantize_mx(out=codes[:].bitcast(FP8X4), scales=scales[:], in_=woven)
            w1_codes[b, a, pair] = codes
            w1_scales[b, a, pair] = scales

        def gather_words(a, half):
            g = keep.tile([P, BANK], U32, name="v_words_%d_%d" % (a, half), align_bytes=64)
            cols = slice(half * BANK // 16, (half + 1) * BANK // 16)
            nc.vector.tensor_copy(g[:], tab_w[a][:].bitcast(U32).indirect(offs_t[:, cols]))
            return g

        for q in range(4):
            rows = slice(QUAD * q, QUAD * q + 8)
            nc.vector.tensor_copy(tab_s[rows, :].bitcast(I32), tab_s_rows[rows, :])
        v_scales = keep.tile([P, S], U8, name="v_scales", align_bytes=64)
        nc.vector.tensor_copy(v_scales[:], tab_s[:].indirect(offs_t[:]))
        v_words = {}
        for a in range(2):
            for half in range(2):
                v_words[a, half] = gather_words(a, half)
        quantize_w1(0, 0, 0, weave_w1(scalar_copy, 0, 0, 0))
        quantize_w1(0, 1, 0, weave_w1(nc.vector.tensor_copy, 0, 1, 0))
        later_pair = [weave_w1(scalar_copy, 0, a, 1) for a in range(2)]

        tilted = {}
        tilted_first = keep.tile([P, LOOK], F32, name="tilted_first")
        best_slot = keep.tile([P, S], F32, name="best")

        def tilt_weights(i):
            t = i % PACK
            if i in (0, 2):
                tw = tilted_first[:]
            elif i == 1:
                tw = best_slot[:, 0:LOOK]
            else:
                tw = grain_t[i - 3][:, 0:LOOK]
            nc.gpsimd.tensor_scalar(
                tw, wgs_t[t // 2][:, LOOK * (t % 2) : LOOK * (t % 2 + 1)], tilt_t[:, i : i + 1], 0.0, ALU.mult, ALU.add
            )
            tilted[i] = tw

        top = keep.tile([P, ROWSETS], F32, name="top")
        look_bias = keep.tile([P, ROWSETS], F32, name="look_bias")
        h_t, look_t, page_t = {}, {}, {}
        size_slots = [keep.tile([P, S], F32, name="size_%d" % k, align_bytes=64) for k in range(3)]
        h_slots = [keep.tile([P, S], F32, name="h_%d" % k) for k in range(3)]
        best_t = [best_slot if i < ROWSETS - 2 else grain_t[i - 1] for i in range(ROWSETS)]
        parts = S // PART
        y_rows = [keep.tile([P, parts, PACK, PART], BF16, name="y_rows_%d" % b) for b in range(2)]
        spans = ((0, 1), (1, 2), (2, 4))
        y_codes, y_scales = {}, {}
        for b in range(2):
            for k, (lo, hi) in enumerate(spans):
                width = PART * (hi - lo)
                if (b, k) != (1, 0):
                    y_codes[b, k] = keep.tile([P, width], U32, name="y_codes_%d_%d" % (b, k), align_bytes=64)[:]
                y_scales[b, k] = keep.tile([P, width], U8, name="y_scales_%d_%d" % (b, k), align_bytes=64)[:]
        y_codes[1, 0] = y_codes[0, 2][:, 0:PART]

        def features(i):
            b, t = divmod(i, PACK)
            pair, cols = t // 2, slice(P * (t % 2), P * (t % 2 + 1))
            size = size_slots[SIZE_SLOT[i]]
            for half in range(2):
                acc = psum.tile([P, BANK], F32, name="acc", tag="banks_1")
                for a in range(2):
                    nc.tensor.matmul_mx(
                        out=acc[:],
                        lhsT=w1_codes[b, a, pair][:, cols].bitcast(FP8X4),
                        lhsT_scale=w1_scales[b, a, pair][:, cols],
                        rhs=v_words[a, half][:].bitcast(FP8X4),
                        rhs_scale=v_scales[4 * a :, BANK * half : BANK * (half + 1)],
                        start=(a == 0),
                        stop=(a == 1),
                    )
                nc.scalar.activation(out=size[:, BANK * half : BANK * (half + 1)], in_=acc[:], func=ACT.Abs)
            h = h_slots[i % 3]
            nc.vector.tensor_scalar(
                h[:], size[:], blank_t[:, i : i + 1], None, ALU.subtract, ALU.max, accum_out=top[:, i : i + 1]
            )
            h_t[i] = h

        def look_and_page(i):
            col = slice(i, i + 1)
            nc.scalar.activation(out=look_bias[:, col], in_=top[:, col], func=ACT.Copy, scale=neg_temp[:, col])
            page = ring.tile([P, S], F32, name="page", bufs=3)
            if i == 0:
                nc.vector.tensor_scalar(page[:], h_t[i][:], skip_t[:, col], None, ALU.mult)
            else:
                nc.scalar.activation(out=page[:], in_=h_t[i][:], func=ACT.Copy, scale=skip_t[:, col])
            look = h_slots[(i - 1) % 3][:, 0:LOOK]
            nc.scalar.activation(
                out=look, in_=h_t[i][:].indirect(pos1_t[:]), func=ACT.Exp, bias=look_bias[:, col], scale=temp_t[:, col]
            )
            look_t[i], page_t[i] = look, page

        def write_page(i):
            tilt_weights(i)
            nc.vector.tensor_tensor(page_t[i][:].indirect(pos2_t[:]), look_t[i], tilted[i], ALU.mult)

        def meet_grain(i, cols):
            nc.vector.tensor_tensor(best_t[i][:, cols], page_t[i][:, cols], grain_t[i][:, cols], ALU.max)

        def apply_gain(i, lo, hi):
            b, t = divmod(i, PACK)
            nc.scalar.activation(
                out=y_rows[b][:, lo:hi, t, :],
                in_=best_t[i][:, PART * lo : PART * hi].rearrange("p (q c) -> p q c", c=PART),
                func=ACT.Copy,
                scale=gain_t[:, i : i + 1],
            )

        def weave_y(engine_copy, b, q, woven):
            engine_copy(
                woven.rearrange("p (c i t) -> p c t i", i=4, t=PACK),
                y_rows[b][:, q, :, :].rearrange("p t (c i) -> p c t i", i=4),
            )

        def woven_tile(name, quarters):
            return keep.tile([P, quarters * PACK * PART], BF16, name=name, align_bytes=64)

        def quantize_y(b, k, woven):
            nc.vector.quantize_mx(out=y_codes[b, k].bitcast(FP8X4), scales=y_scales[b, k], in_=woven)

        quarter = PACK * PART
        woven_q = [woven_tile("y_woven_q%d" % q, 1) for q in range(2)]
        woven_half = [woven_tile("y_woven_half%d" % b, 2) for b in range(2)]

        features(0)
        features(1)
        for a in range(2):
            quantize_w1(0, a, 1, later_pair[a])
        look_and_page(0)
        write_page(0)
        last = ROWSETS - 1
        for r in range(last):
            if r + 2 < ROWSETS:
                features(r + 2)
            look_and_page(r + 1)
            if r + 1 < last:
                write_page(r + 1)
            if r in (0, 1):
                late = size_slots[r + 1][:].bitcast(BF16).rearrange("p (a c) -> p a c", a=2)
            if r == 0:
                for a in range(2):
                    quantize_w1(1, a, 0, weave_w1(scalar_copy, 1, a, 0, late[:, a, :]))
            if r in (1, 2):
                quantize_w1(1, r - 1, 1, weave_w1(scalar_copy, 1, r - 1, 1, late[:, r - 1, :]))
            if r == 5:
                weave_y(nc.scalar.copy, 0, 1, woven_q[1][:])
                quantize_y(0, 1, woven_q[1][:])
            if r == 6:
                for q in (2, 3):
                    weave_y(nc.scalar.copy, 0, q, woven_half[0][:, quarter * (q - 2) : quarter * (q - 1)])
            if r >= 1:
                apply_gain(r - 1, 0, parts)
            meet_grain(r, slice(0, S))
            if r == 4:
                weave_y(nc.scalar.copy, 0, 0, woven_q[0][:])
                quantize_y(0, 0, woven_q[0][:])
        write_page(last)
        apply_gain(last - 1, 0, parts)

        banks = [(k, n, 2) for k in range(2) for n in range(0, N // P, 2)] + [(2, n, 1) for n in range(N // P)]
        sums = {}

        def read_out(g, b):
            k, n0, count = banks[g]
            if b == 0:
                sums[g] = psum.tile([P, BANK], F32, name="sums", tag="banks_%d" % (g // 4 % 2))
            width = BANK // count
            for m in range(count):
                n = n0 + m
                nc.tensor.matmul_mx(
                    out=sums[g][:, width * m : width * (m + 1)],
                    lhsT=w2_w[:, b, 2 * P * n : 2 * P * (n + 1)].bitcast(FP4X4),
                    lhsT_scale=w2_s[:, b, P * n : P * (n + 1)],
                    rhs=y_codes[b, k].bitcast(FP8X4),
                    rhs_scale=y_scales[b, k],
                    start=(b == 0 and m == 0),
                    stop=(b == 1 and m == count - 1),
                )

        def store(g, engine_copy):
            k, n0, count = banks[g]
            staged = ring.tile([P, BANK], F32, name="staged", bufs=12)
            engine_copy(staged[:], sums[g][:])
            lo, hi = spans[k]
            nc.sync.dma_start(
                out=out[P * n0 : P * (n0 + count), PART * lo : PART * hi].rearrange("(m p) c -> p m c", p=P),
                in_=staged[:].rearrange("p (m c) -> p m c", m=count),
            )

        for g in range(6):
            read_out(g, 0)
        for q in range(parts):
            meet_grain(last, slice(PART * q, PART * (q + 1)))
            apply_gain(last, q, q + 1)
        weave_y(nc.vector.tensor_copy, 1, 0, woven_half[1][:, 0:quarter])
        quantize_y(1, 0, woven_half[1][:, 0:quarter])
        weave_y(nc.scalar.copy, 1, 1, woven_q[1][:])
        for g in range(3):
            read_out(g, 1)
            store(g, nc.scalar.copy)
        nc.vector.tensor_copy(
            woven_half[1][:].rearrange("p (q c i t) -> p q c t i", q=2, i=4, t=PACK),
            y_rows[1][:, 2:4, :, :].rearrange("p q t (c i) -> p q c t i", i=4),
        )
        quantize_y(1, 1, woven_q[1][:])
        quantize_y(0, 2, woven_half[0][:])
        quantize_y(1, 2, woven_half[1][:])
        for g in range(3, len(banks)):
            if g >= 6:
                read_out(g, 0)
            read_out(g, 1)
            store(g, nc.vector.tensor_copy if g in (6, 7, 9, 11) else nc.scalar.copy)
